import numpy as np
import ml_dtypes


def mxq(x, axis, fmt="e4m3"):
    dtype, down = {"e4m3": (ml_dtypes.float8_e4m3fn, 7), "e5m2": (ml_dtypes.float8_e5m2, 14)}[fmt]
    v = np.moveaxis(np.asarray(x, np.float32).astype(ml_dtypes.bfloat16).astype(np.float64), axis, -1)
    blocks = v.reshape(v.shape[:-1] + (-1, 32))
    amax = np.abs(blocks).max(-1, keepdims=True)
    byte = np.maximum(np.where(amax > 0, np.frexp(amax)[1] - 1 + 127, 0) - down, 1)
    scale = np.exp2(byte - 127.0)
    codes = (blocks / scale).astype(np.float32).astype(dtype).astype(np.float64)
    return np.moveaxis((codes * scale).reshape(v.shape), -1, axis)


WIDE = False


def mx_kscale(k, group=512):
    if not WIDE:
        return np.ones(k)
    levels = np.array([10, -10, 5, -5, 0])
    if group != 512:
        return np.exp2(np.random.permutation(np.resize(levels, k // group))).repeat(group)
    if k % 512:
        return np.exp2(np.random.permutation(np.resize(levels, k // 32))).repeat(32)
    a = np.empty((k // 512, 16))
    for p in range(k // 512):
        a[p, :8] = np.random.permutation(np.resize(levels, 8))
        for g in range(8):
            far = levels[np.abs(levels - a[p, g]) >= 10]
            a[p, g + 8] = far[np.random.randint(len(far))]
    return np.exp2(a.ravel()).repeat(32)


def f64(x):
    return np.asarray(x).astype(np.float64)


def striped(idx):
    return np.tile(np.asarray(idx).reshape(-1, 16).T, (8, 1)).astype(np.uint16)


def unstriped(offs):
    return offs[:16].T.reshape(-1).astype(np.int64)


H, KV, D, NQ, N = 4, 4, 256, 512, 512


def setup_inputs():
    n = np.random.standard_normal
    s = mx_kscale(D, 0)[:, None]
    u = mx_kscale(N)
    t = np.random.uniform(0.5, 2.0, N) * u
    v = n((KV, N, 128))
    v[:, :, 127] = 1.0
    return {
        "qT": (n((H, D, NQ)) * s * (0.70 / np.sqrt(D))).astype(np.float32),
        "kT": (n((KV, D, N)) / s).astype(np.float32),
        "t": t.reshape(N, 1).astype(np.float32),
        "v": (v / t[:, None]).astype(np.float32),
        "kb": (0.5 * n((N, 1))).astype(np.float32),
        "og": n((H, NQ, 128)).astype(np.float32),
    }


def reference(qT, kT, t, v, kb, og):
    a = mxq(f64(kT), 1, "e4m3").transpose(0, 2, 1) @ mxq(f64(qT), 1, "e4m3")
    a = a + f64(kb)
    p = np.exp(a)
    w = p * f64(t)
    y = mxq(w, 1, "e4m3").transpose(0, 2, 1) @ mxq(f64(v), 1, "e4m3")
    y = y / (y[:, :, 127:128])
    y = y / (1.0 + np.exp(-f64(og)))
    return y

@@ -1,0 +1,239 @@
+from contextlib import ExitStack
+
+import math
+
+import concourse.mybir as mybir
+
+H, D, NQ, N, E = 4, 256, 512, 512, 128
+FLOPS = 2 * H * N * NQ * D + 2 * H * NQ * N * E
+
+F32 = mybir.dt.float32
+BF16 = mybir.dt.bfloat16
+U32 = mybir.dt.uint32
+I32 = mybir.dt.int32
+U8 = mybir.dt.uint8
+FP8X4 = mybir.dt.float8_e4m3fn_x4
+ALU = mybir.AluOpType
+ACT = mybir.ActivationFunctionType
+
+P = 128
+PACK = 4
+ROWS = 64
+TILE = 128
+
+
+def tile_rows_a_exp_kb_gate_kernel(tc, qT, kT, t, v, kb, og, out):
+    nc = tc.nc
+    with ExitStack() as ctx:
+        sb = ctx.enter_context(tc.tile_pool(name="sb", bufs=1))
+        ps = ctx.enter_context(tc.psum_pool(name="ps", bufs=1))
+        ctx.enter_context(tc.manual_schedule())
+
+        def new(shape, dtype, name):
+            return sb.tile(shape, dtype, name=name, align_bytes=64)
+
+        t_sb = new([P, PACK], F32, "t_sb")
+        kb_sb = new([P, PACK], F32, "kb_sb")
+        nc.sync.dma_start(out=t_sb[:], in_=t.rearrange("(p j) o -> p (j o)", j=PACK))
+        q_raw = [new([P, PACK, NQ], F32, "q_raw%d" % g) for g in range(2)]
+        k_raw = [new([P, PACK, N], F32, "k_raw%d" % g) for g in range(2)]
+        for g in range(2):
+            nc.sync.dma_start(out=q_raw[g][:], in_=qT[2 * g : 2 * g + 2].rearrange("h (p j) n -> (h p) j n", j=PACK))
+            if g == 0:
+                nc.sync.dma_start(out=kb_sb[:], in_=kb.rearrange("(p j) o -> p (j o)", j=PACK))
+            nc.sync.dma_start(out=k_raw[g][:], in_=kT[2 * g : 2 * g + 2].rearrange("h (p j) n -> (h p) j n", j=PACK))
+        v_raw = new([P, H, PACK * E], F32, "v_raw")
+        nc.sync.dma_start(out=v_raw[:], in_=v.rearrange("h (p j) e -> p h (j e)", j=PACK))
+        og_sb = new([P, H, PACK * E], F32, "og_sb")
+        nc.sync.dma_start(out=og_sb[:], in_=og.rearrange("h (m c) e -> m h (c e)", c=PACK))
+
+        t_abs = new([P, PACK], F32, "t_abs")
+        nc.vector.scalar_tensor_tensor(out=t_abs[:], in0=t_sb[:], scalar=-1.0, in1=t_sb[:], op0=ALU.mult, op1=ALU.max)
+        t_pos = new([P, PACK], F32, "t_pos")
+        nc.vector.tensor_scalar(out=t_pos[:], in0=t_sb[:], scalar1=0.0, scalar2=2.0, op0=ALU.is_ge, op1=ALU.mult)
+        log_t = [new([P, PACK], F32, "log_t%d" % i) for i in range(4)]
+        nc.vector.tensor_scalar(
+            out=log_t[0][:], in0=t_abs[:].bitcast(I32), scalar1=math.log(2.0) / 2.0**23, scalar2=0.03 - 127.0 * math.log(2.0),
+            op0=ALU.mult, op1=ALU.add,
+        )
+        t_sign = new([P, PACK], BF16, "t_sign")
+        nc.vector.tensor_scalar(out=t_sign[:], in0=t_pos[:], scalar1=-1.0, scalar2=None, op0=ALU.add)
+        bias = new([P, PACK], F32, "bias")
+
+        def newton_step(i):
+            inverse = new([P, PACK], F32, "inverse%d" % i)
+            nc.scalar.activation(out=inverse[:], in_=log_t[i][:], func=ACT.Exp, scale=-1.0)
+            ratio = new([P, PACK], F32, "ratio%d" % i)
+            nc.vector.tensor_tensor(out=ratio[:], in0=inverse[:], in1=t_abs[:], op=ALU.mult)
+            nc.vector.scalar_tensor_tensor(
+                out=log_t[i + 1][:], in0=ratio[:], scalar=-1.0, in1=log_t[i][:], op0=ALU.add, op1=ALU.add
+            )
+
+        def copy_on(engine, out_ap, in_ap):
+            if engine == "vector":
+                nc.vector.tensor_copy(out=out_ap, in_=in_ap)
+            else:
+                nc.scalar.copy(out=out_ap, in_=in_ap)
+
+        def deal(engine, grouped, raw, s0, s1, r0, r1):
+            copy_on(
+                engine,
+                grouped[:, r0:r1, s0:s1, :].rearrange("p r s j -> p s j r"),
+                raw[:].rearrange("p j (s r) -> p s j r", r=PACK)[:, s0:s1, :, r0:r1],
+            )
+
+        def operand(name):
+            return (
+                new([P, PACK, TILE, PACK], BF16, name + "_bf"),
+                new([P, PACK * TILE], U32, name + "_codes"),
+                new([P, PACK * TILE], U8, name + "_scales"),
+            )
+
+        def quantize(op, r0, r1):
+            grouped, codes, scales = op
+            cols = slice(r0 * TILE, r1 * TILE)
+            nc.vector.quantize_mx(
+                out=codes[:, cols].bitcast(FP8X4),
+                scales=scales[:, cols],
+                in_=grouped[:, r0:r1].rearrange("p r s j -> p (r s j)"),
+            )
+
+        q_op = [operand("q%d" % g) for g in range(2)]
+        k_op = [operand("k%d" % g) for g in range(2)]
+        v_op = operand("v")
+        w_op = [operand("w%d" % h) for h in range(H)]
+        w_rows = [new([P, PACK, NQ], BF16, "w_rows%d" % h) for h in range(H)]
+        score = {}
+
+        def scores(h, r):
+            g, rows = h // 2, slice(ROWS * (h % 2), ROWS * (h % 2 + 1))
+            bank = ps.tile([P, NQ], F32, name="score%d_%d" % (h, r), tag="score%d" % (h % 2), bufs=3)
+            score[h, r] = bank
+            tok = slice(r * TILE, (r + 1) * TILE)
+            for c in range(PACK):
+                qry = slice(c * TILE, (c + 1) * TILE)
+                nc.tensor.matmul_mx(
+                    out=bank[:, qry],
+                    lhsT=k_op[g][1][rows, tok].bitcast(FP8X4),
+                    lhsT_scale=k_op[g][2][rows, tok],
+                    rhs=q_op[g][1][rows, qry].bitcast(FP8X4),
+                    rhs_scale=q_op[g][2][rows, qry],
+                    start=True,
+                    stop=True,
+                )
+
+        def weigh(h, r):
+            nc.scalar.activation(out=w_rows[h][:, r, :], in_=score[h, r][:], func=ACT.Exp, bias=bias[:, r : r + 1])
+
+        def interleave_w(engine, h):
+            copy_on(
+                engine,
+                w_op[h][0][:].rearrange("p c (a i) r -> p (c a) r i", i=4),
+                w_rows[h][:].rearrange("p r (a i) -> p a r i", i=4),
+            )
+
+        y = {}
+
+        def second_product(h):
+            bank = ps.tile([P, PACK, E], F32, name="y%d" % h, tag="y", bufs=2)
+            y[h] = bank
+            feat = slice(h * E, (h + 1) * E)
+            for c in range(PACK):
+                qry = slice(c * TILE, (c + 1) * TILE)
+                nc.tensor.matmul_mx(
+                    out=bank[:, c, :],
+                    lhsT=w_op[h][1][:, qry].bitcast(FP8X4),
+                    lhsT_scale=w_op[h][2][:, qry],
+                    rhs=v_op[1][:, feat].bitcast(FP8X4),
+                    rhs_scale=v_op[2][:, feat],
+                    start=True,
+                    stop=True,
+                )
+
+        gate = new([P, H, PACK * E], F32, "gate")
+        gated = [new([P, PACK, E], F32, "gated%d" % h) for h in range(H)]
+        result = [new([P, PACK, E], F32, "result%d" % h) for h in range(H)]
+        inv = [new([P, PACK], F32, "inv%d" % h) for h in range(H)]
+        half_inv = [new([P, PACK], F32, "half_inv%d" % h) for h in range(H)]
+
+        def gate_y(h):
+            nc.vector.reciprocal(out=inv[h][:], in_=y[h][:, :, E - 1])
+            nc.vector.scalar_tensor_tensor(
+                out=gated[h][:].rearrange("p c e -> p (c e)"),
+                in0=gate[:, h, :],
+                scalar=1.0,
+                in1=y[h][:].rearrange("p c e -> p (c e)"),
+                op0=ALU.add,
+                op1=ALU.mult,
+            )
+            nc.vector.tensor_scalar(out=half_inv[h][:], in0=inv[h][:], scalar1=0.5, scalar2=None, op0=ALU.mult)
+
+        def divide(engine, h):
+            for c in range(PACK):
+                if engine == "vector":
+                    nc.vector.tensor_scalar(
+                        out=result[h][:, c, :], in0=gated[h][:, c, :], scalar1=half_inv[h][:, c : c + 1], scalar2=None, op0=ALU.mult
+                    )
+                else:
+                    nc.scalar.activation(
+                        out=result[h][:, c, :], in_=gated[h][:, c, :], func=ACT.Copy, scale=half_inv[h][:, c : c + 1]
+                    )
+            nc.sync.dma_start(out=out[h].rearrange("(m c) e -> m c e", c=PACK), in_=result[h][:])
+
+        newton_step(0)
+        newton_step(1)
+        deal("vector", q_op[0][0], q_raw[0], 0, TILE, 0, 4)
+        newton_step(2)
+        quantize(q_op[0], 0, 4)
+        nc.vector.tensor_tensor(out=bias[:], in0=log_t[3][:], in1=kb_sb[:], op=ALU.add)
+        deal("vector", k_op[0][0], k_raw[0], 0, TILE, 0, 2)
+        deal("scalar", k_op[0][0], k_raw[0], 0, TILE, 2, 4)
+        quantize(k_op[0], 0, 2)
+        quantize(k_op[0], 2, 4)
+        deal("vector", q_op[1][0], q_raw[1], 0, TILE, 0, 4)
+        quantize(q_op[1], 0, 4)
+        deal("vector", k_op[1][0], k_raw[1], 0, TILE, 0, 2)
+        deal("vector", k_op[1][0], k_raw[1], 0, TILE, 2, 4)
+        quantize(k_op[1], 0, 2)
+        quantize(k_op[1], 2, 4)
+        steps = [(h, r) for h in range(H) for r in range(PACK)]
+        for i in range(len(steps) + 3):
+            if i >= 3:
+                weigh(*steps[i - 3])
+            if i < len(steps):
+                scores(*steps[i])
+        interleave_w("scalar", 3)
+        for h in range(H):
+            nc.scalar.activation(out=gate[:, h, :], in_=og_sb[:, h, :], func=ACT.Tanh, scale=0.5)
+        interleave_w("vector", 0)
+        interleave_w("vector", 1)
+        quantize(w_op[0], 0, 4)
+        quantize(w_op[1], 0, 4)
+
+        v_plain = new([P, H, E, PACK], BF16, "v_plain")
+        nc.vector.tensor_copy(
+            out=v_plain[:].rearrange("p h (a i) j -> p h a j i", i=4),
+            in_=v_raw[:].rearrange("p h (j a i) -> p h a j i", j=PACK, i=4),
+        )
+        interleave_w("vector", 2)
+        nc.vector.tensor_tensor(
+            out=v_op[0][:].rearrange("p h e j -> p (h e) j"),
+            in0=v_plain[:].rearrange("p h e j -> p (h e) j"),
+            in1=t_sign[:].unsqueeze(1).to_broadcast([P, H * E, PACK]),
+            op=ALU.mult,
+        )
+        quantize(w_op[2], 0, 4)
+        quantize(v_op, 0, 4)
+        second_product(0)
+        second_product(1)
+        quantize(w_op[3], 0, 4)
+        gate_y(0)
+        second_product(2)
+        divide("scalar", 0)
+        gate_y(1)
+        second_product(3)
+        divide("scalar", 1)
+        gate_y(2)
+        divide("scalar", 2)
+        gate_y(3)
+        divide("vector", 3)

@@ -60,13 +60,18 @@ def tile_rows_a_exp_kb_gate_kernel(tc, qT, kT, t, v, kb, og, out):
         nc.vector.tensor_scalar(out=t_sign[:], in0=t_pos[:], scalar1=-1.0, scalar2=None, op0=ALU.add)
         bias = new([P, PACK], F32, "bias")
 
-        def newton_step(i):
-            inverse = new([P, PACK], F32, "inverse%d" % i)
-            nc.scalar.activation(out=inverse[:], in_=log_t[i][:], func=ACT.Exp, scale=-1.0)
-            ratio = new([P, PACK], F32, "ratio%d" % i)
-            nc.vector.tensor_tensor(out=ratio[:], in0=inverse[:], in1=t_abs[:], op=ALU.mult)
+        ratio = [new([P, PACK], F32, "ratio%d" % i) for i in range(3)]
+        inverse = [new([P, PACK], F32, "inverse%d" % i) for i in range(3)]
+
+        def newton_exp(i):
+            nc.scalar.activation(out=inverse[i][:], in_=log_t[i][:], func=ACT.Exp, scale=-1.0)
+
+        def newton_ratio(i):
+            nc.vector.tensor_tensor(out=ratio[i][:], in0=inverse[i][:], in1=t_abs[:], op=ALU.mult)
+
+        def newton_update(i):
             nc.vector.scalar_tensor_tensor(
-                out=log_t[i + 1][:], in0=ratio[:], scalar=-1.0, in1=log_t[i][:], op0=ALU.add, op1=ALU.add
+                out=log_t[i + 1][:], in0=ratio[i][:], scalar=-1.0, in1=log_t[i][:], op0=ALU.add, op1=ALU.add
             )
 
         def copy_on(engine, out_ap, in_ap):
@@ -75,52 +80,55 @@ def tile_rows_a_exp_kb_gate_kernel(tc, qT, kT, t, v, kb, og, out):
             else:
                 nc.scalar.copy(out=out_ap, in_=in_ap)
 
-        def deal(engine, grouped, raw, s0, s1, r0, r1):
+        def deal(engine, op, raw, part=0):
+            count = PACK // len(op[0])
             copy_on(
                 engine,
-                grouped[:, r0:r1, s0:s1, :].rearrange("p r s j -> p s j r"),
-                raw[:].rearrange("p j (s r) -> p s j r", r=PACK)[:, s0:s1, :, r0:r1],
+                op[0][part][:].rearrange("p r s j -> p s j r"),
+                raw[:].rearrange("p j (s r) -> p s j r", r=PACK)[:, :, :, part * count : (part + 1) * count],
             )
 
-        def operand(name):
+        def operand(name, parts=1):
             return (
-                new([P, PACK, TILE, PACK], BF16, name + "_bf"),
+                [new([P, PACK // parts, TILE, PACK], BF16, "%s_bf%d" % (name, i)) for i in range(parts)],
                 new([P, PACK * TILE], U32, name + "_codes"),
                 new([P, PACK * TILE], U8, name + "_scales"),
             )
 
-        def quantize(op, r0, r1):
+        def quantize(op, part=0):
             grouped, codes, scales = op
-            cols = slice(r0 * TILE, r1 * TILE)
+            width = PACK * TILE // len(grouped)
+            cols = slice(part * width, (part + 1) * width)
             nc.vector.quantize_mx(
                 out=codes[:, cols].bitcast(FP8X4),
                 scales=scales[:, cols],
-                in_=grouped[:, r0:r1].rearrange("p r s j -> p (r s j)"),
+                in_=grouped[part][:].rearrange("p r s j -> p (r s j)"),
             )
 
         q_op = [operand("q%d" % g) for g in range(2)]
-        k_op = [operand("k%d" % g) for g in range(2)]
+        k_op = [operand("k%d" % g, 2) for g in range(2)]
         v_op = operand("v")
         w_op = [operand("w%d" % h) for h in range(H)]
         w_rows = [new([P, PACK, NQ], BF16, "w_rows%d" % h) for h in range(H)]
         score = {}
 
-        def scores(h, r):
-            g, rows = h // 2, slice(ROWS * (h % 2), ROWS * (h % 2 + 1))
-            bank = ps.tile([P, NQ], F32, name="score%d_%d" % (h, r), tag="score%d" % (h % 2), bufs=3)
-            score[h, r] = bank
+        def scores(g, r):
             tok = slice(r * TILE, (r + 1) * TILE)
+            for side in range(2):
+                score[2 * g + side, r] = ps.tile([P, NQ], F32, name="score%d_%d" % (2 * g + side, r), tag="score%d" % side, bufs=3)
             for c in range(PACK):
                 qry = slice(c * TILE, (c + 1) * TILE)
-                nc.tensor.matmul_mx(
-                    out=bank[:, qry],
-                    lhsT=k_op[g][1][rows, tok].bitcast(FP8X4),
-                    lhsT_scale=k_op[g][2][rows, tok],
-                    rhs=q_op[g][1][rows, qry].bitcast(FP8X4),
-                    rhs_scale=q_op[g][2][rows, qry],
-                    start=True,
-                    stop=True,
-                )
+                for side in range(2):
+                    rows = slice(ROWS * side, ROWS * (side + 1))
+                    nc.tensor.matmul_mx(
+                        out=score[2 * g + side, r][:, qry],
+                        lhsT=k_op[g][1][rows, tok].bitcast(FP8X4),
+                        lhsT_scale=k_op[g][2][rows, tok],
+                        rhs=q_op[g][1][rows, qry].bitcast(FP8X4),
+                        rhs_scale=q_op[g][2][rows, qry],
+                        start=True,
+                        stop=True,
+                    )
 
         def weigh(h, r):
             nc.scalar.activation(out=w_rows[h][:, r, :], in_=score[h, r][:], func=ACT.Exp, bias=bias[:, r : r + 1])
@@ -128,7 +136,7 @@ def tile_rows_a_exp_kb_gate_kernel(tc, qT, kT, t, v, kb, og, out):
         def interleave_w(engine, h):
             copy_on(
                 engine,
-                w_op[h][0][:].rearrange("p c (a i) r -> p (c a) r i", i=4),
+                w_op[h][0][0][:].rearrange("p c (a i) r -> p (c a) r i", i=4),
                 w_rows[h][:].rearrange("p r (a i) -> p a r i", i=4),
             )
 
@@ -156,84 +164,104 @@ def tile_rows_a_exp_kb_gate_kernel(tc, qT, kT, t, v, kb, og, out):
         inv = [new([P, PACK], F32, "inv%d" % h) for h in range(H)]
         half_inv = [new([P, PACK], F32, "half_inv%d" % h) for h in range(H)]
 
-        def gate_y(h):
+        def invert(h):
             nc.vector.reciprocal(out=inv[h][:], in_=y[h][:, :, E - 1])
+
+        def gate_y(h, c0, c1):
             nc.vector.scalar_tensor_tensor(
-                out=gated[h][:].rearrange("p c e -> p (c e)"),
-                in0=gate[:, h, :],
+                out=gated[h][:, c0:c1].rearrange("p c e -> p (c e)"),
+                in0=gate[:, h, c0 * E : c1 * E],
                 scalar=1.0,
-                in1=y[h][:].rearrange("p c e -> p (c e)"),
+                in1=y[h][:, c0:c1].rearrange("p c e -> p (c e)"),
                 op0=ALU.add,
                 op1=ALU.mult,
             )
-            nc.vector.tensor_scalar(out=half_inv[h][:], in0=inv[h][:], scalar1=0.5, scalar2=None, op0=ALU.mult)
 
-        def divide(engine, h):
+        def store(h, c0, c1):
+            nc.sync.dma_start(out=out[h].rearrange("(m c) e -> m c e", c=PACK)[:, c0:c1], in_=result[h][:, c0:c1])
+
+        def divide_on_scalar(h):
+            nc.scalar.activation(out=half_inv[h][:], in_=inv[h][:], func=ACT.Copy, scale=0.5)
             for c in range(PACK):
-                if engine == "vector":
-                    nc.vector.tensor_scalar(
-                        out=result[h][:, c, :], in0=gated[h][:, c, :], scalar1=half_inv[h][:, c : c + 1], scalar2=None, op0=ALU.mult
-                    )
-                else:
-                    nc.scalar.activation(
-                        out=result[h][:, c, :], in_=gated[h][:, c, :], func=ACT.Copy, scale=half_inv[h][:, c : c + 1]
-                    )
-            nc.sync.dma_start(out=out[h].rearrange("(m c) e -> m c e", c=PACK), in_=result[h][:])
+                nc.scalar.activation(out=result[h][:, c, :], in_=gated[h][:, c, :], func=ACT.Copy, scale=half_inv[h][:, c : c + 1])
+            store(h, 0, PACK)
 
-        newton_step(0)
-        newton_step(1)
-        deal("vector", q_op[0][0], q_raw[0], 0, TILE, 0, 4)
-        newton_step(2)
-        quantize(q_op[0], 0, 4)
+        def divide_on_vector(h, c0, c1):
+            for c in range(c0, c1):
+                nc.vector.tensor_scalar(
+                    out=result[h][:, c, :], in0=gated[h][:, c, :], scalar1=inv[h][:, c : c + 1], scalar2=0.5, op0=ALU.mult, op1=ALU.mult
+                )
+            store(h, c0, c1)
+
+        def tanh_gate(h):
+            nc.scalar.activation(out=gate[:, h, :], in_=og_sb[:, h, :], func=ACT.Tanh, scale=0.5)
+
+        newton_exp(0)
+        newton_ratio(0)
+        newton_update(0)
+        newton_exp(1)
+        deal("vector", q_op[0], q_raw[0])
+        newton_ratio(1)
+        newton_update(1)
+        quantize(q_op[0])
+        newton_exp(2)
+        deal("vector", k_op[0], k_raw[0])
+        deal("scalar", k_op[0], k_raw[0], 1)
+        newton_ratio(2)
+        quantize(k_op[0])
+        newton_update(2)
         nc.vector.tensor_tensor(out=bias[:], in0=log_t[3][:], in1=kb_sb[:], op=ALU.add)
-        deal("vector", k_op[0][0], k_raw[0], 0, TILE, 0, 2)
-        deal("scalar", k_op[0][0], k_raw[0], 0, TILE, 2, 4)
-        quantize(k_op[0], 0, 2)
-        quantize(k_op[0], 2, 4)
-        deal("vector", q_op[1][0], q_raw[1], 0, TILE, 0, 4)
-        quantize(q_op[1], 0, 4)
-        deal("vector", k_op[1][0], k_raw[1], 0, TILE, 0, 2)
-        deal("vector", k_op[1][0], k_raw[1], 0, TILE, 2, 4)
-        quantize(k_op[1], 0, 2)
-        quantize(k_op[1], 2, 4)
-        steps = [(h, r) for h in range(H) for r in range(PACK)]
+        quantize(k_op[0], 1)
+        deal("vector", q_op[1], q_raw[1])
+        quantize(q_op[1])
+        deal("vector", k_op[1], k_raw[1])
+        deal("vector", k_op[1], k_raw[1], 1)
+        quantize(k_op[1])
+        quantize(k_op[1], 1)
+        steps = [(g, r) for g in range(2) for r in range(PACK)]
         for i in range(len(steps) + 3):
             if i >= 3:
-                weigh(*steps[i - 3])
+                g, r = steps[i - 3]
+                weigh(2 * g, r)
+                weigh(2 * g + 1, r)
             if i < len(steps):
                 scores(*steps[i])
+        tanh_gate(0)
+        tanh_gate(1)
         interleave_w("scalar", 3)
-        for h in range(H):
-            nc.scalar.activation(out=gate[:, h, :], in_=og_sb[:, h, :], func=ACT.Tanh, scale=0.5)
-        interleave_w("vector", 0)
-        interleave_w("vector", 1)
-        quantize(w_op[0], 0, 4)
-        quantize(w_op[1], 0, 4)
 
         v_plain = new([P, H, E, PACK], BF16, "v_plain")
         nc.vector.tensor_copy(
             out=v_plain[:].rearrange("p h (a i) j -> p h a j i", i=4),
             in_=v_raw[:].rearrange("p h (j a i) -> p h a j i", j=PACK, i=4),
         )
-        interleave_w("vector", 2)
+        interleave_w("vector", 0)
         nc.vector.tensor_tensor(
-            out=v_op[0][:].rearrange("p h e j -> p (h e) j"),
+            out=v_op[0][0][:].rearrange("p h e j -> p (h e) j"),
             in0=v_plain[:].rearrange("p h e j -> p (h e) j"),
             in1=t_sign[:].unsqueeze(1).to_broadcast([P, H * E, PACK]),
             op=ALU.mult,
         )
-        quantize(w_op[2], 0, 4)
-        quantize(v_op, 0, 4)
+        interleave_w("vector", 1)
+        quantize(v_op)
+        quantize(w_op[0])
+        quantize(w_op[1])
         second_product(0)
         second_product(1)
-        quantize(w_op[3], 0, 4)
-        gate_y(0)
-        second_product(2)
-        divide("scalar", 0)
-        gate_y(1)
-        second_product(3)
-        divide("scalar", 1)
-        gate_y(2)
-        divide("scalar", 2)
-        gate_y(3)
-        divide("vector", 3)
+        interleave_w("vector", 2)
+        for h in range(2):
+            invert(h)
+            gate_y(h, 0, 4)
+            divide_on_scalar(h)
+        for h in range(2, 4):
+            quantize(w_op[h])
+            second_product(h)
+            tanh_gate(h)
+        invert(2)
+        gate_y(2, 0, 4)
+        divide_on_scalar(2)
+        invert(3)
+        gate_y(3, 0, 2)
+        gate_y(3, 2, 4)
+        divide_on_vector(3, 0, 2)
+        divide_on_vector(3, 2, 4)

@@ -112,23 +112,22 @@ def tile_rows_a_exp_kb_gate_kernel(tc, qT, kT, t, v, kb, og, out):
         w_rows = [new([P, PACK, NQ], BF16, "w_rows%d" % h) for h in range(H)]
         score = {}
 
-        def scores(g, r):
+        def scores(h, r):
+            g, rows = h // 2, slice(ROWS * (h % 2), ROWS * (h % 2 + 1))
+            bank = ps.tile([P, NQ], F32, name="score%d_%d" % (h, r), tag="score%d" % (h % 2), bufs=2)
+            score[h, r] = bank
             tok = slice(r * TILE, (r + 1) * TILE)
-            for side in range(2):
-                score[2 * g + side, r] = ps.tile([P, NQ], F32, name="score%d_%d" % (2 * g + side, r), tag="score%d" % side, bufs=3)
             for c in range(PACK):
                 qry = slice(c * TILE, (c + 1) * TILE)
-                for side in range(2):
-                    rows = slice(ROWS * side, ROWS * (side + 1))
-                    nc.tensor.matmul_mx(
-                        out=score[2 * g + side, r][:, qry],
-                        lhsT=k_op[g][1][rows, tok].bitcast(FP8X4),
-                        lhsT_scale=k_op[g][2][rows, tok],
-                        rhs=q_op[g][1][rows, qry].bitcast(FP8X4),
-                        rhs_scale=q_op[g][2][rows, qry],
-                        start=True,
-                        stop=True,
-                    )
+                nc.tensor.matmul_mx(
+                    out=bank[:, qry],
+                    lhsT=k_op[g][1][rows, tok].bitcast(FP8X4),
+                    lhsT_scale=k_op[g][2][rows, tok],
+                    rhs=q_op[g][1][rows, qry].bitcast(FP8X4),
+                    rhs_scale=q_op[g][2][rows, qry],
+                    start=True,
+                    stop=True,
+                )
 
         def weigh(h, r):
             nc.scalar.activation(out=w_rows[h][:, r, :], in_=score[h, r][:], func=ACT.Exp, bias=bias[:, r : r + 1])
@@ -143,7 +142,7 @@ def tile_rows_a_exp_kb_gate_kernel(tc, qT, kT, t, v, kb, og, out):
         y = {}
 
         def second_product(h):
-            bank = ps.tile([P, PACK, E], F32, name="y%d" % h, tag="y", bufs=2)
+            bank = ps.tile([P, PACK, E], F32, name="y%d" % h, tag="y", bufs=4)
             y[h] = bank
             feat = slice(h * E, (h + 1) * E)
             for c in range(PACK):
@@ -167,6 +166,9 @@ def tile_rows_a_exp_kb_gate_kernel(tc, qT, kT, t, v, kb, og, out):
         def invert(h):
             nc.vector.reciprocal(out=inv[h][:], in_=y[h][:, :, E - 1])
 
+        def halve(h):
+            nc.vector.tensor_scalar(out=half_inv[h][:], in0=inv[h][:], scalar1=0.5, scalar2=None, op0=ALU.mult)
+
         def gate_y(h, c0, c1):
             nc.vector.scalar_tensor_tensor(
                 out=gated[h][:, c0:c1].rearrange("p c e -> p (c e)"),
@@ -180,11 +182,10 @@ def tile_rows_a_exp_kb_gate_kernel(tc, qT, kT, t, v, kb, og, out):
         def store(h, c0, c1):
             nc.sync.dma_start(out=out[h].rearrange("(m c) e -> m c e", c=PACK)[:, c0:c1], in_=result[h][:, c0:c1])
 
-        def divide_on_scalar(h):
-            nc.scalar.activation(out=half_inv[h][:], in_=inv[h][:], func=ACT.Copy, scale=0.5)
-            for c in range(PACK):
+        def divide_on_scalar(h, c0, c1):
+            for c in range(c0, c1):
                 nc.scalar.activation(out=result[h][:, c, :], in_=gated[h][:, c, :], func=ACT.Copy, scale=half_inv[h][:, c : c + 1])
-            store(h, 0, PACK)
+            store(h, c0, c1)
 
         def divide_on_vector(h, c0, c1):
             for c in range(c0, c1):
@@ -218,49 +219,53 @@ def tile_rows_a_exp_kb_gate_kernel(tc, qT, kT, t, v, kb, og, out):
         deal("vector", k_op[1], k_raw[1], 1)
         quantize(k_op[1])
         quantize(k_op[1], 1)
-        steps = [(g, r) for g in range(2) for r in range(PACK)]
-        for i in range(len(steps) + 3):
-            if i >= 3:
-                g, r = steps[i - 3]
-                weigh(2 * g, r)
-                weigh(2 * g + 1, r)
+        steps = sorted(((h, r) for h in range(H) for r in range(PACK)), key=lambda hr: (hr[0] // 2, 2 * hr[1] + 3 * (hr[0] % 2)))
+        for i in range(len(steps) + 2):
+            if i >= 2:
+                weigh(*steps[i - 2])
             if i < len(steps):
                 scores(*steps[i])
         tanh_gate(0)
-        tanh_gate(1)
         interleave_w("scalar", 3)
+        tanh_gate(1)
+        tanh_gate(2)
 
         v_plain = new([P, H, E, PACK], BF16, "v_plain")
+        interleave_w("vector", 0)
         nc.vector.tensor_copy(
             out=v_plain[:].rearrange("p h (a i) j -> p h a j i", i=4),
             in_=v_raw[:].rearrange("p h (j a i) -> p h a j i", j=PACK, i=4),
         )
-        interleave_w("vector", 0)
+        interleave_w("vector", 1)
         nc.vector.tensor_tensor(
             out=v_op[0][0][:].rearrange("p h e j -> p (h e) j"),
             in0=v_plain[:].rearrange("p h e j -> p (h e) j"),
             in1=t_sign[:].unsqueeze(1).to_broadcast([P, H * E, PACK]),
             op=ALU.mult,
         )
-        interleave_w("vector", 1)
-        quantize(v_op)
         quantize(w_op[0])
-        quantize(w_op[1])
+        quantize(v_op)
         second_product(0)
-        second_product(1)
         interleave_w("vector", 2)
-        for h in range(2):
-            invert(h)
-            gate_y(h, 0, 4)
-            divide_on_scalar(h)
-        for h in range(2, 4):
-            quantize(w_op[h])
-            second_product(h)
-            tanh_gate(h)
+        quantize(w_op[1])
+        second_product(1)
+        invert(0)
+        gate_y(0, 0, 4)
+        halve(0)
+        divide_on_scalar(0, 0, 4)
+        tanh_gate(3)
+        quantize(w_op[2])
+        second_product(2)
+        invert(1)
+        quantize(w_op[3])
+        second_product(3)
+        gate_y(1, 0, 4)
+        halve(1)
+        divide_on_scalar(1, 0, 4)
         invert(2)
         gate_y(2, 0, 4)
-        divide_on_scalar(2)
         invert(3)
+        divide_on_vector(2, 0, 4)
         gate_y(3, 0, 2)
         gate_y(3, 2, 4)
         divide_on_vector(3, 0, 2)

@@ -1,6 +1,5 @@
-from contextlib import ExitStack
-
 import math
+from contextlib import ExitStack
 
 import concourse.mybir as mybir
 
@@ -18,8 +17,13 @@ ACT = mybir.ActivationFunctionType
 
 P = 128
 PACK = 4
-ROWS = 64
+ROWS = D // PACK
 TILE = 128
+PAIRS = H // 2
+RUN = 4
+SCORE_BANKS = 2
+NEWTON_STEPS = 3
+GUESS_CENTRE = 0.03
 
 
 def tile_rows_a_exp_kb_gate_kernel(tc, qT, kT, t, v, kb, og, out):
@@ -34,58 +38,50 @@ def tile_rows_a_exp_kb_gate_kernel(tc, qT, kT, t, v, kb, og, out):
 
         t_sb = new([P, PACK], F32, "t_sb")
         kb_sb = new([P, PACK], F32, "kb_sb")
-        nc.sync.dma_start(out=t_sb[:], in_=t.rearrange("(p j) o -> p (j o)", j=PACK))
-        q_raw = [new([P, PACK, NQ], F32, "q_raw%d" % g) for g in range(2)]
-        k_raw = [new([P, PACK, N], F32, "k_raw%d" % g) for g in range(2)]
-        for g in range(2):
-            nc.sync.dma_start(out=q_raw[g][:], in_=qT[2 * g : 2 * g + 2].rearrange("h (p j) n -> (h p) j n", j=PACK))
-            if g == 0:
-                nc.sync.dma_start(out=kb_sb[:], in_=kb.rearrange("(p j) o -> p (j o)", j=PACK))
-            nc.sync.dma_start(out=k_raw[g][:], in_=kT[2 * g : 2 * g + 2].rearrange("h (p j) n -> (h p) j n", j=PACK))
+        q_raw = [new([P, PACK, NQ], F32, "q_raw%d" % g) for g in range(PAIRS)]
+        k_raw = [new([P, PACK, N], F32, "k_raw%d" % g) for g in range(PAIRS)]
+
+        def load_pair(raw, src, g):
+            nc.sync.dma_start(out=raw[g][:], in_=src[2 * g : 2 * g + 2].rearrange("h (p j) n -> (h p) j n", j=PACK))
+
+        nc.scalar.dma_start(out=t_sb[:], in_=t.rearrange("(p j) o -> p (j o)", j=PACK))
+        nc.scalar.dma_start(out=kb_sb[:], in_=kb.rearrange("(p j) o -> p (j o)", j=PACK))
+        for g in range(PAIRS):
+            load_pair(q_raw, qT, g)
+            load_pair(k_raw, kT, g)
         v_raw = new([P, H, PACK * E], F32, "v_raw")
         nc.sync.dma_start(out=v_raw[:], in_=v.rearrange("h (p j) e -> p h (j e)", j=PACK))
         og_sb = new([P, H, PACK * E], F32, "og_sb")
-        nc.sync.dma_start(out=og_sb[:], in_=og.rearrange("h (m c) e -> m h (c e)", c=PACK))
+        nc.sync.dma_start(out=og_sb[:], in_=og.rearrange("h (s c) e -> s h (c e)", c=PACK))
 
         t_abs = new([P, PACK], F32, "t_abs")
         nc.vector.scalar_tensor_tensor(out=t_abs[:], in0=t_sb[:], scalar=-1.0, in1=t_sb[:], op0=ALU.mult, op1=ALU.max)
-        t_pos = new([P, PACK], F32, "t_pos")
-        nc.vector.tensor_scalar(out=t_pos[:], in0=t_sb[:], scalar1=0.0, scalar2=2.0, op0=ALU.is_ge, op1=ALU.mult)
-        log_t = [new([P, PACK], F32, "log_t%d" % i) for i in range(4)]
+        t_step = new([P, PACK], F32, "t_step")
+        nc.vector.tensor_scalar(out=t_step[:], in0=t_sb[:], scalar1=0.0, scalar2=2.0, op0=ALU.is_ge, op1=ALU.mult)
+        log_t = [new([P, PACK], F32, "log_t%d" % i) for i in range(NEWTON_STEPS + 1)]
         nc.vector.tensor_scalar(
-            out=log_t[0][:], in0=t_abs[:].bitcast(I32), scalar1=math.log(2.0) / 2.0**23, scalar2=0.03 - 127.0 * math.log(2.0),
-            op0=ALU.mult, op1=ALU.add,
+            out=log_t[0][:],
+            in0=t_abs[:].bitcast(I32),
+            scalar1=math.log(2.0) / 2.0**23,
+            scalar2=GUESS_CENTRE - 127.0 * math.log(2.0),
+            op0=ALU.mult,
+            op1=ALU.add,
         )
         t_sign = new([P, PACK], BF16, "t_sign")
-        nc.vector.tensor_scalar(out=t_sign[:], in0=t_pos[:], scalar1=-1.0, scalar2=None, op0=ALU.add)
+        nc.vector.tensor_scalar(out=t_sign[:], in0=t_step[:], scalar1=-1.0, scalar2=None, op0=ALU.add)
         bias = new([P, PACK], F32, "bias")
-
-        ratio = [new([P, PACK], F32, "ratio%d" % i) for i in range(3)]
-        inverse = [new([P, PACK], F32, "inverse%d" % i) for i in range(3)]
+        ratio = [new([P, PACK], F32, "ratio%d" % i) for i in range(NEWTON_STEPS)]
+        exp_minus = [new([P, PACK], F32, "exp_minus%d" % i) for i in range(NEWTON_STEPS)]
 
         def newton_exp(i):
-            nc.scalar.activation(out=inverse[i][:], in_=log_t[i][:], func=ACT.Exp, scale=-1.0)
+            nc.scalar.activation(out=exp_minus[i][:], in_=log_t[i][:], func=ACT.Exp, scale=-1.0)
 
         def newton_ratio(i):
-            nc.vector.tensor_tensor(out=ratio[i][:], in0=inverse[i][:], in1=t_abs[:], op=ALU.mult)
+            nc.vector.tensor_tensor(out=ratio[i][:], in0=exp_minus[i][:], in1=t_abs[:], op=ALU.mult)
 
         def newton_update(i):
             nc.vector.scalar_tensor_tensor(
                 out=log_t[i + 1][:], in0=ratio[i][:], scalar=-1.0, in1=log_t[i][:], op0=ALU.add, op1=ALU.add
-            )
-
-        def copy_on(engine, out_ap, in_ap):
-            if engine == "vector":
-                nc.vector.tensor_copy(out=out_ap, in_=in_ap)
-            else:
-                nc.scalar.copy(out=out_ap, in_=in_ap)
-
-        def deal(engine, op, raw, part=0):
-            count = PACK // len(op[0])
-            copy_on(
-                engine,
-                op[0][part][:].rearrange("p r s j -> p s j r"),
-                raw[:].rearrange("p j (s r) -> p s j r", r=PACK)[:, :, :, part * count : (part + 1) * count],
             )
 
         def operand(name, parts=1):
@@ -105,16 +101,26 @@ def tile_rows_a_exp_kb_gate_kernel(tc, qT, kT, t, v, kb, og, out):
                 in_=grouped[part][:].rearrange("p r s j -> p (r s j)"),
             )
 
-        q_op = [operand("q%d" % g) for g in range(2)]
-        k_op = [operand("k%d" % g, 2) for g in range(2)]
+        def deal(copy, op, raw, part=0):
+            grouped = op[0]
+            count = PACK // len(grouped)
+            copy(
+                out=grouped[part][:].rearrange("p r s j -> p s j r"),
+                in_=raw[:].rearrange("p j (s r) -> p s j r", r=PACK)[:, :, :, part * count : (part + 1) * count],
+            )
+
+        q_op = [operand("q%d" % g) for g in range(PAIRS)]
+        k_op = [operand("k%d" % g, 2) for g in range(PAIRS)]
         v_op = operand("v")
         w_op = [operand("w%d" % h) for h in range(H)]
         w_rows = [new([P, PACK, NQ], BF16, "w_rows%d" % h) for h in range(H)]
+
         score = {}
 
         def scores(h, r):
-            g, rows = h // 2, slice(ROWS * (h % 2), ROWS * (h % 2 + 1))
-            bank = ps.tile([P, NQ], F32, name="score%d_%d" % (h, r), tag="score%d" % (h % 2), bufs=2)
+            g, side = divmod(h, 2)
+            rows = slice(ROWS * side, ROWS * (side + 1))
+            bank = ps.tile([P, NQ], F32, name="score%d_%d" % (h, r), tag="score%d" % side, bufs=SCORE_BANKS)
             score[h, r] = bank
             tok = slice(r * TILE, (r + 1) * TILE)
             for c in range(PACK):
@@ -132,17 +138,16 @@ def tile_rows_a_exp_kb_gate_kernel(tc, qT, kT, t, v, kb, og, out):
         def weigh(h, r):
             nc.scalar.activation(out=w_rows[h][:, r, :], in_=score[h, r][:], func=ACT.Exp, bias=bias[:, r : r + 1])
 
-        def interleave_w(engine, h):
-            copy_on(
-                engine,
-                w_op[h][0][0][:].rearrange("p c (a i) r -> p (c a) r i", i=4),
-                w_rows[h][:].rearrange("p r (a i) -> p a r i", i=4),
+        def interleave_w(copy, h):
+            copy(
+                out=w_op[h][0][0][:].rearrange("p c (a i) r -> p (c a) r i", i=RUN),
+                in_=w_rows[h][:].rearrange("p r (a i) -> p a r i", i=RUN),
             )
 
         y = {}
 
         def second_product(h):
-            bank = ps.tile([P, PACK, E], F32, name="y%d" % h, tag="y", bufs=4)
+            bank = ps.tile([P, PACK, E], F32, name="y%d" % h, tag="y", bufs=H)
             y[h] = bank
             feat = slice(h * E, (h + 1) * E)
             for c in range(PACK):
@@ -157,116 +162,128 @@ def tile_rows_a_exp_kb_gate_kernel(tc, qT, kT, t, v, kb, og, out):
                     stop=True,
                 )
 
-        gate = new([P, H, PACK * E], F32, "gate")
+        tanh_og = new([P, H, PACK * E], F32, "tanh_og")
         gated = [new([P, PACK, E], F32, "gated%d" % h) for h in range(H)]
         result = [new([P, PACK, E], F32, "result%d" % h) for h in range(H)]
         inv = [new([P, PACK], F32, "inv%d" % h) for h in range(H)]
-        half_inv = [new([P, PACK], F32, "half_inv%d" % h) for h in range(H)]
+
+        def tanh_gate(h):
+            nc.scalar.activation(out=tanh_og[:, h, :], in_=og_sb[:, h, :], func=ACT.Tanh, scale=0.5)
 
         def invert(h):
             nc.vector.reciprocal(out=inv[h][:], in_=y[h][:, :, E - 1])
 
-        def halve(h):
-            nc.vector.tensor_scalar(out=half_inv[h][:], in0=inv[h][:], scalar1=0.5, scalar2=None, op0=ALU.mult)
-
-        def gate_y(h, c0, c1):
+        def gate_y(h, c0=0, c1=PACK):
             nc.vector.scalar_tensor_tensor(
                 out=gated[h][:, c0:c1].rearrange("p c e -> p (c e)"),
-                in0=gate[:, h, c0 * E : c1 * E],
+                in0=tanh_og[:, h, c0 * E : c1 * E],
                 scalar=1.0,
                 in1=y[h][:, c0:c1].rearrange("p c e -> p (c e)"),
                 op0=ALU.add,
                 op1=ALU.mult,
             )
 
-        def store(h, c0, c1):
-            nc.sync.dma_start(out=out[h].rearrange("(m c) e -> m c e", c=PACK)[:, c0:c1], in_=result[h][:, c0:c1])
+        def store(h, c0=0, c1=PACK):
+            nc.sync.dma_start(out=out[h].rearrange("(s c) e -> s c e", c=PACK)[:, c0:c1], in_=result[h][:, c0:c1])
 
-        def divide_on_scalar(h, c0, c1):
-            for c in range(c0, c1):
-                nc.scalar.activation(out=result[h][:, c, :], in_=gated[h][:, c, :], func=ACT.Copy, scale=half_inv[h][:, c : c + 1])
-            store(h, c0, c1)
+        def divide_on_scalar(h):
+            half_inv = new([P, PACK], F32, "half_inv%d" % h)
+            nc.vector.tensor_scalar(out=half_inv[:], in0=inv[h][:], scalar1=0.5, scalar2=None, op0=ALU.mult)
+            for c in range(PACK):
+                nc.scalar.activation(
+                    out=result[h][:, c, :], in_=gated[h][:, c, :], func=ACT.Copy, scale=half_inv[:, c : c + 1]
+                )
+            store(h)
 
-        def divide_on_vector(h, c0, c1):
+        def divide_on_vector(h, c0=0, c1=PACK):
             for c in range(c0, c1):
                 nc.vector.tensor_scalar(
-                    out=result[h][:, c, :], in0=gated[h][:, c, :], scalar1=inv[h][:, c : c + 1], scalar2=0.5, op0=ALU.mult, op1=ALU.mult
+                    out=result[h][:, c, :],
+                    in0=gated[h][:, c, :],
+                    scalar1=inv[h][:, c : c + 1],
+                    scalar2=0.5,
+                    op0=ALU.mult,
+                    op1=ALU.mult,
                 )
             store(h, c0, c1)
 
-        def tanh_gate(h):
-            nc.scalar.activation(out=gate[:, h, :], in_=og_sb[:, h, :], func=ACT.Tanh, scale=0.5)
+        on_vector, on_scalar = nc.vector.tensor_copy, nc.scalar.copy
 
         newton_exp(0)
         newton_ratio(0)
         newton_update(0)
         newton_exp(1)
-        deal("vector", q_op[0], q_raw[0])
+        deal(on_vector, q_op[0], q_raw[0])
         newton_ratio(1)
         newton_update(1)
         quantize(q_op[0])
         newton_exp(2)
-        deal("vector", k_op[0], k_raw[0])
-        deal("scalar", k_op[0], k_raw[0], 1)
+        deal(on_vector, k_op[0], k_raw[0], 0)
+        deal(on_scalar, k_op[0], k_raw[0], 1)
         newton_ratio(2)
-        quantize(k_op[0])
+        quantize(k_op[0], 0)
         newton_update(2)
-        nc.vector.tensor_tensor(out=bias[:], in0=log_t[3][:], in1=kb_sb[:], op=ALU.add)
+        nc.vector.tensor_tensor(out=bias[:], in0=log_t[NEWTON_STEPS][:], in1=kb_sb[:], op=ALU.add)
         quantize(k_op[0], 1)
-        deal("vector", q_op[1], q_raw[1])
+
+        deal(on_vector, q_op[1], q_raw[1])
         quantize(q_op[1])
-        deal("vector", k_op[1], k_raw[1])
-        deal("vector", k_op[1], k_raw[1], 1)
-        quantize(k_op[1])
-        quantize(k_op[1], 1)
-        steps = sorted(((h, r) for h in range(H) for r in range(PACK)), key=lambda hr: (hr[0] // 2, 2 * hr[1] + 3 * (hr[0] % 2)))
-        for i in range(len(steps) + 2):
-            if i >= 2:
-                weigh(*steps[i - 2])
+        for part in range(2):
+            deal(on_vector, k_op[1], k_raw[1], part)
+        for part in range(2):
+            quantize(k_op[1], part)
+
+        steps = sorted(
+            ((h, r) for h in range(H) for r in range(PACK)), key=lambda hr: (hr[0] // 2, 2 * hr[1] + 3 * (hr[0] % 2))
+        )
+        for i in range(len(steps) + SCORE_BANKS):
+            if i >= SCORE_BANKS:
+                weigh(*steps[i - SCORE_BANKS])
             if i < len(steps):
                 scores(*steps[i])
+
         tanh_gate(0)
-        interleave_w("scalar", 3)
+        interleave_w(on_scalar, 3)
         tanh_gate(1)
         tanh_gate(2)
 
-        v_plain = new([P, H, E, PACK], BF16, "v_plain")
-        interleave_w("vector", 0)
+        v_unsigned = new([P, H, E, PACK], BF16, "v_unsigned")
+        interleave_w(on_vector, 0)
         nc.vector.tensor_copy(
-            out=v_plain[:].rearrange("p h (a i) j -> p h a j i", i=4),
-            in_=v_raw[:].rearrange("p h (j a i) -> p h a j i", j=PACK, i=4),
+            out=v_unsigned[:].rearrange("p h (a i) j -> p h a j i", i=RUN),
+            in_=v_raw[:].rearrange("p h (j a i) -> p h a j i", j=PACK, i=RUN),
         )
-        interleave_w("vector", 1)
+        interleave_w(on_vector, 1)
         nc.vector.tensor_tensor(
             out=v_op[0][0][:].rearrange("p h e j -> p (h e) j"),
-            in0=v_plain[:].rearrange("p h e j -> p (h e) j"),
+            in0=v_unsigned[:].rearrange("p h e j -> p (h e) j"),
             in1=t_sign[:].unsqueeze(1).to_broadcast([P, H * E, PACK]),
             op=ALU.mult,
         )
         quantize(w_op[0])
         quantize(v_op)
         second_product(0)
-        interleave_w("vector", 2)
+        interleave_w(on_vector, 2)
         quantize(w_op[1])
         second_product(1)
+
         invert(0)
-        gate_y(0, 0, 4)
-        halve(0)
-        divide_on_scalar(0, 0, 4)
+        gate_y(0)
+        divide_on_scalar(0)
         tanh_gate(3)
         quantize(w_op[2])
         second_product(2)
         invert(1)
         quantize(w_op[3])
         second_product(3)
-        gate_y(1, 0, 4)
-        halve(1)
-        divide_on_scalar(1, 0, 4)
+        gate_y(1)
+        divide_on_scalar(1)
         invert(2)
-        gate_y(2, 0, 4)
+        gate_y(2)
         invert(3)
-        divide_on_vector(2, 0, 4)
-        gate_y(3, 0, 2)
-        gate_y(3, 2, 4)
-        divide_on_vector(3, 0, 2)
-        divide_on_vector(3, 2, 4)
+        divide_on_vector(2)
+        halves = ((0, PACK // 2), (PACK // 2, PACK))
+        for c0, c1 in halves:
+            gate_y(3, c0, c1)
+        for c0, c1 in halves:
+            divide_on_vector(3, c0, c1)

import math
from contextlib import ExitStack

import concourse.mybir as mybir

H, D, NQ, N, E = 4, 256, 512, 512, 128
FLOPS = 2 * H * N * NQ * D + 2 * H * NQ * N * E

F32 = mybir.dt.float32
BF16 = mybir.dt.bfloat16
U32 = mybir.dt.uint32
I32 = mybir.dt.int32
U8 = mybir.dt.uint8
FP8X4 = mybir.dt.float8_e4m3fn_x4
ALU = mybir.AluOpType
ACT = mybir.ActivationFunctionType

P = 128
PACK = 4
ROWS = D // PACK
TILE = 128
PAIRS = H // 2
RUN = 4
SCORE_BANKS = 2
NEWTON_STEPS = 3
GUESS_CENTRE = 0.03


def tile_rows_a_exp_kb_gate_kernel(tc, qT, kT, t, v, kb, og, out):
    nc = tc.nc
    with ExitStack() as ctx:
        sb = ctx.enter_context(tc.tile_pool(name="sb", bufs=1))
        ps = ctx.enter_context(tc.psum_pool(name="ps", bufs=1))
        ctx.enter_context(tc.manual_schedule())

        def new(shape, dtype, name):
            return sb.tile(shape, dtype, name=name, align_bytes=64)

        t_sb = new([P, PACK], F32, "t_sb")
        kb_sb = new([P, PACK], F32, "kb_sb")
        q_raw = [new([P, PACK, NQ], F32, "q_raw%d" % g) for g in range(PAIRS)]
        k_raw = [new([P, PACK, N], F32, "k_raw%d" % g) for g in range(PAIRS)]

        def load_pair(raw, src, g):
            nc.sync.dma_start(out=raw[g][:], in_=src[2 * g : 2 * g + 2].rearrange("h (p j) n -> (h p) j n", j=PACK))

        nc.scalar.dma_start(out=t_sb[:], in_=t.rearrange("(p j) o -> p (j o)", j=PACK))
        nc.scalar.dma_start(out=kb_sb[:], in_=kb.rearrange("(p j) o -> p (j o)", j=PACK))
        for g in range(PAIRS):
            load_pair(q_raw, qT, g)
            load_pair(k_raw, kT, g)
        v_raw = new([P, H, PACK * E], F32, "v_raw")
        nc.sync.dma_start(out=v_raw[:], in_=v.rearrange("h (p j) e -> p h (j e)", j=PACK))
        og_sb = new([P, H, PACK * E], F32, "og_sb")
        nc.sync.dma_start(out=og_sb[:], in_=og.rearrange("h (s c) e -> s h (c e)", c=PACK))

        t_abs = new([P, PACK], F32, "t_abs")
        nc.vector.scalar_tensor_tensor(out=t_abs[:], in0=t_sb[:], scalar=-1.0, in1=t_sb[:], op0=ALU.mult, op1=ALU.max)
        t_step = new([P, PACK], F32, "t_step")
        nc.vector.tensor_scalar(out=t_step[:], in0=t_sb[:], scalar1=0.0, scalar2=2.0, op0=ALU.is_ge, op1=ALU.mult)
        log_t = [new([P, PACK], F32, "log_t%d" % i) for i in range(NEWTON_STEPS + 1)]
        nc.vector.tensor_scalar(
            out=log_t[0][:],
            in0=t_abs[:].bitcast(I32),
            scalar1=math.log(2.0) / 2.0**23,
            scalar2=GUESS_CENTRE - 127.0 * math.log(2.0),
            op0=ALU.mult,
            op1=ALU.add,
        )
        t_sign = new([P, PACK], BF16, "t_sign")
        nc.vector.tensor_scalar(out=t_sign[:], in0=t_step[:], scalar1=-1.0, scalar2=None, op0=ALU.add)
        bias = new([P, PACK], F32, "bias")
        ratio = [new([P, PACK], F32, "ratio%d" % i) for i in range(NEWTON_STEPS)]
        exp_minus = [new([P, PACK], F32, "exp_minus%d" % i) for i in range(NEWTON_STEPS)]

        def newton_exp(i):
            nc.scalar.activation(out=exp_minus[i][:], in_=log_t[i][:], func=ACT.Exp, scale=-1.0)

        def newton_ratio(i):
            nc.vector.tensor_tensor(out=ratio[i][:], in0=exp_minus[i][:], in1=t_abs[:], op=ALU.mult)

        def newton_update(i):
            nc.vector.scalar_tensor_tensor(
                out=log_t[i + 1][:], in0=ratio[i][:], scalar=-1.0, in1=log_t[i][:], op0=ALU.add, op1=ALU.add
            )

        def operand(name, parts=1):
            return (
                [new([P, PACK // parts, TILE, PACK], BF16, "%s_bf%d" % (name, i)) for i in range(parts)],
                new([P, PACK * TILE], U32, name + "_codes"),
                new([P, PACK * TILE], U8, name + "_scales"),
            )

        def quantize(op, part=0):
            grouped, codes, scales = op
            width = PACK * TILE // len(grouped)
            cols = slice(part * width, (part + 1) * width)
            nc.vector.quantize_mx(
                out=codes[:, cols].bitcast(FP8X4),
                scales=scales[:, cols],
                in_=grouped[part][:].rearrange("p r s j -> p (r s j)"),
            )

        def deal(copy, op, raw, part=0):
            grouped = op[0]
            count = PACK // len(grouped)
            copy(
                out=grouped[part][:].rearrange("p r s j -> p s j r"),
                in_=raw[:].rearrange("p j (s r) -> p s j r", r=PACK)[:, :, :, part * count : (part + 1) * count],
            )

        q_op = [operand("q%d" % g) for g in range(PAIRS)]
        k_op = [operand("k%d" % g, 2) for g in range(PAIRS)]
        v_op = operand("v")
        w_op = [operand("w%d" % h) for h in range(H)]
        w_rows = [new([P, PACK, NQ], BF16, "w_rows%d" % h) for h in range(H)]

        score = {}

        def scores(h, r):
            g, side = divmod(h, 2)
            rows = slice(ROWS * side, ROWS * (side + 1))
            bank = ps.tile([P, NQ], F32, name="score%d_%d" % (h, r), tag="score%d" % side, bufs=SCORE_BANKS)
            score[h, r] = bank
            tok = slice(r * TILE, (r + 1) * TILE)
            for c in range(PACK):
                qry = slice(c * TILE, (c + 1) * TILE)
                nc.tensor.matmul_mx(
                    out=bank[:, qry],
                    lhsT=k_op[g][1][rows, tok].bitcast(FP8X4),
                    lhsT_scale=k_op[g][2][rows, tok],
                    rhs=q_op[g][1][rows, qry].bitcast(FP8X4),
                    rhs_scale=q_op[g][2][rows, qry],
                    start=True,
                    stop=True,
                )

        def weigh(h, r):
            nc.scalar.activation(out=w_rows[h][:, r, :], in_=score[h, r][:], func=ACT.Exp, bias=bias[:, r : r + 1])

        def interleave_w(copy, h):
            copy(
                out=w_op[h][0][0][:].rearrange("p c (a i) r -> p (c a) r i", i=RUN),
                in_=w_rows[h][:].rearrange("p r (a i) -> p a r i", i=RUN),
            )

        y = {}

        def second_product(h):
            bank = ps.tile([P, PACK, E], F32, name="y%d" % h, tag="y", bufs=H)
            y[h] = bank
            feat = slice(h * E, (h + 1) * E)
            for c in range(PACK):
                qry = slice(c * TILE, (c + 1) * TILE)
                nc.tensor.matmul_mx(
                    out=bank[:, c, :],
                    lhsT=w_op[h][1][:, qry].bitcast(FP8X4),
                    lhsT_scale=w_op[h][2][:, qry],
                    rhs=v_op[1][:, feat].bitcast(FP8X4),
                    rhs_scale=v_op[2][:, feat],
                    start=True,
                    stop=True,
                )

        tanh_og = new([P, H, PACK * E], F32, "tanh_og")
        gated = [new([P, PACK, E], F32, "gated%d" % h) for h in range(H)]
        result = [new([P, PACK, E], F32, "result%d" % h) for h in range(H)]
        inv = [new([P, PACK], F32, "inv%d" % h) for h in range(H)]

        def tanh_gate(h):
            nc.scalar.activation(out=tanh_og[:, h, :], in_=og_sb[:, h, :], func=ACT.Tanh, scale=0.5)

        def invert(h):
            nc.vector.reciprocal(out=inv[h][:], in_=y[h][:, :, E - 1])

        def gate_y(h, c0=0, c1=PACK):
            nc.vector.scalar_tensor_tensor(
                out=gated[h][:, c0:c1].rearrange("p c e -> p (c e)"),
                in0=tanh_og[:, h, c0 * E : c1 * E],
                scalar=1.0,
                in1=y[h][:, c0:c1].rearrange("p c e -> p (c e)"),
                op0=ALU.add,
                op1=ALU.mult,
            )

        def store(h, c0=0, c1=PACK):
            nc.sync.dma_start(out=out[h].rearrange("(s c) e -> s c e", c=PACK)[:, c0:c1], in_=result[h][:, c0:c1])

        def divide_on_scalar(h):
            half_inv = new([P, PACK], F32, "half_inv%d" % h)
            nc.vector.tensor_scalar(out=half_inv[:], in0=inv[h][:], scalar1=0.5, scalar2=None, op0=ALU.mult)
            for c in range(PACK):
                nc.scalar.activation(
                    out=result[h][:, c, :], in_=gated[h][:, c, :], func=ACT.Copy, scale=half_inv[:, c : c + 1]
                )
            store(h)

        def divide_on_vector(h, c0=0, c1=PACK):
            for c in range(c0, c1):
                nc.vector.tensor_scalar(
                    out=result[h][:, c, :],
                    in0=gated[h][:, c, :],
                    scalar1=inv[h][:, c : c + 1],
                    scalar2=0.5,
                    op0=ALU.mult,
                    op1=ALU.mult,
                )
            store(h, c0, c1)

        on_vector, on_scalar = nc.vector.tensor_copy, nc.scalar.copy

        newton_exp(0)
        newton_ratio(0)
        newton_update(0)
        newton_exp(1)
        deal(on_vector, q_op[0], q_raw[0])
        newton_ratio(1)
        newton_update(1)
        quantize(q_op[0])
        newton_exp(2)
        deal(on_vector, k_op[0], k_raw[0], 0)
        deal(on_scalar, k_op[0], k_raw[0], 1)
        newton_ratio(2)
        quantize(k_op[0], 0)
        newton_update(2)
        nc.vector.tensor_tensor(out=bias[:], in0=log_t[NEWTON_STEPS][:], in1=kb_sb[:], op=ALU.add)
        quantize(k_op[0], 1)

        deal(on_vector, q_op[1], q_raw[1])
        quantize(q_op[1])
        for part in range(2):
            deal(on_vector, k_op[1], k_raw[1], part)
        for part in range(2):
            quantize(k_op[1], part)

        steps = sorted(
            ((h, r) for h in range(H) for r in range(PACK)), key=lambda hr: (hr[0] // 2, 2 * hr[1] + 3 * (hr[0] % 2))
        )
        for i in range(len(steps) + SCORE_BANKS):
            if i >= SCORE_BANKS:
                weigh(*steps[i - SCORE_BANKS])
            if i < len(steps):
                scores(*steps[i])

        tanh_gate(0)
        interleave_w(on_scalar, 3)
        tanh_gate(1)
        tanh_gate(2)

        v_unsigned = new([P, H, E, PACK], BF16, "v_unsigned")
        interleave_w(on_vector, 0)
        nc.vector.tensor_copy(
            out=v_unsigned[:].rearrange("p h (a i) j -> p h a j i", i=RUN),
            in_=v_raw[:].rearrange("p h (j a i) -> p h a j i", j=PACK, i=RUN),
        )
        interleave_w(on_vector, 1)
        nc.vector.tensor_tensor(
            out=v_op[0][0][:].rearrange("p h e j -> p (h e) j"),
            in0=v_unsigned[:].rearrange("p h e j -> p (h e) j"),
            in1=t_sign[:].unsqueeze(1).to_broadcast([P, H * E, PACK]),
            op=ALU.mult,
        )
        quantize(w_op[0])
        quantize(v_op)
        second_product(0)
        interleave_w(on_vector, 2)
        quantize(w_op[1])
        second_product(1)

        invert(0)
        gate_y(0)
        divide_on_scalar(0)
        tanh_gate(3)
        quantize(w_op[2])
        second_product(2)
        invert(1)
        quantize(w_op[3])
        second_product(3)
        gate_y(1)
        divide_on_scalar(1)
        invert(2)
        gate_y(2)
        invert(3)
        divide_on_vector(2)
        halves = ((0, PACK // 2), (PACK // 2, PACK))
        for c0, c1 in halves:
            gate_y(3, c0, c1)
        for c0, c1 in halves:
            divide_on_vector(3, c0, c1)
